import numpy as np
import ml_dtypes


def mxq(x, axis, fmt="e4m3"):
    dtype, down = {"e4m3": (ml_dtypes.float8_e4m3fn, 7), "e5m2": (ml_dtypes.float8_e5m2, 14)}[fmt]
    v = np.moveaxis(np.asarray(x, np.float32).astype(ml_dtypes.bfloat16).astype(np.float64), axis, -1)
    blocks = v.reshape(v.shape[:-1] + (-1, 32))
    amax = np.abs(blocks).max(-1, keepdims=True)
    byte = np.maximum(np.where(amax > 0, np.frexp(amax)[1] - 1 + 127, 0) - down, 1)
    scale = np.exp2(byte - 127.0)
    codes = (blocks / scale).astype(np.float32).astype(dtype).astype(np.float64)
    return np.moveaxis((codes * scale).reshape(v.shape), -1, axis)


WIDE = False


def mx_kscale(k):
    if not WIDE:
        return np.ones(k)
    levels = np.array([30, -30])
    if k % 512:
        return np.exp2(np.random.permutation(np.resize(levels, k // 32))).repeat(32)
    a = np.empty((k // 512, 16))
    for p in range(k // 512):
        a[p, :8] = np.random.permutation(np.resize(levels, 8))
        for g in range(8):
            far = levels[np.abs(levels - a[p, g]) >= 10]
            a[p, g + 8] = far[np.random.randint(len(far))]
    return np.exp2(a.ravel()).repeat(32)


def f64(x):
    return np.asarray(x).astype(np.float64)


def striped(idx):
    return np.tile(np.asarray(idx).reshape(-1, 16).T, (8, 1)).astype(np.uint16)


def unstriped(offs):
    return offs[:16].T.reshape(-1).astype(np.int64)


E2M1 = np.array([0.0, 0.5, 1.0, 1.5, 2.0, 3.0, 4.0, 6.0, -0.0, -0.5, -1.0, -1.5, -2.0, -3.0, -4.0, -6.0])


def pack_weight(w, fmt):
    k, n = w.shape
    w = f64(np.asarray(w, np.float32).astype(ml_dtypes.bfloat16)).reshape(k // 32, 32, n)
    amax = np.abs(w).max(1)
    if fmt in ("e4m3", "e5m2"):
        byte = np.frexp(amax)[1] - 1 + 127 - (7 if fmt == "e4m3" else 14)
    else:
        mant, ex = np.frexp(amax / 6.0)
        byte = np.where(mant > 0.5, ex, ex - 1) + 127
    byte = np.clip(np.where(amax > 0, byte, 1), 1, 254)
    scaled = (w * np.exp2(127.0 - byte)[:, None, :]).reshape(k, n).astype(np.float32)
    by_word = np.ascontiguousarray(scaled.reshape(k // 512, 128, 4, n).transpose(0, 1, 3, 2))
    if fmt in ("e4m3", "e5m2"):
        words = by_word.astype(ml_dtypes.float8_e4m3fn if fmt == "e4m3" else ml_dtypes.float8_e5m2).view(np.uint8)
    else:
        c = by_word.astype(ml_dtypes.float4_e2m1fn).view(np.uint8) & 0xF
        words = (c[..., 0::2] | (c[..., 1::2] << 4)).reshape(k // 512, 128, 2 * n)
    return np.ascontiguousarray(words), np.ascontiguousarray(byte.astype(np.uint8).reshape(k // 512, 16, n))


def unpack_weight(words, scales, fmt):
    g, _, n = scales.shape
    words = np.ascontiguousarray(words).reshape(g, 128, n, -1)
    if fmt in ("e4m3", "e5m2"):
        vals = words.view(ml_dtypes.float8_e4m3fn if fmt == "e4m3" else ml_dtypes.float8_e5m2).astype(np.float64)
    else:
        nib = np.empty((g, 128, n, 4), np.uint8)
        nib[..., 0::2] = words & 0xF
        nib[..., 1::2] = words >> 4
        vals = E2M1[nib]
    vals = vals * np.repeat(np.exp2(scales.astype(np.float64) - 127.0), 8, axis=1)[..., None]
    return vals.transpose(0, 1, 3, 2).reshape(g * 512, n)


K, T, J, R, C, N, E = 512, 2048, 256, 512, 512, 256, 128


def setup_inputs():
    n = np.random.standard_normal
    idx = np.random.permutation(T)[:J]
    idx2 = np.random.permutation(T)[:J]
    idx3 = np.random.permutation(C)[:J]
    idx4 = np.random.permutation(C)[:J]
    idx5 = np.random.permutation(J)[:E]
    idx6 = np.random.permutation(J)[:E]
    fk = mx_kscale(K)
    fr = mx_kscale(R)
    xtp = pack_weight(n((K, T)) / fk[:, None], "e5m2")
    wp = pack_weight(n((K, R)) * 1 / np.sqrt(K) * fk[:, None] * fr, "e2m1")
    wbp = pack_weight(n((R, N)) * 1 / np.sqrt(R) / fr[:, None], "e2m1")
    wsp = pack_weight(n((K, N)) * 1 / np.sqrt(K) * fk[:, None], "e2m1")
    return {
        "xt_words": xtp[0],
        "xt_scales": xtp[1],
        "w_words": wp[0],
        "w_scales": wp[1],
        "wb_words": wbp[0],
        "wb_scales": wbp[1],
        "ws_words": wsp[0],
        "ws_scales": wsp[1],
        "offs": striped(idx),
        "offs2": striped(idx2),
        "offs3": striped(idx3),
        "offs4": striped(idx4),
        "offs5": striped(idx5),
        "offs6": striped(idx6),
    }


def reference(xt_words, xt_scales, w_words, w_scales, wb_words, wb_scales, ws_words, ws_scales, offs, offs2, offs3, offs4, offs5, offs6):
    idx = unstriped(offs)
    idx2 = unstriped(offs2)
    idx3 = unstriped(offs3)
    idx4 = unstriped(offs4)
    idx5 = unstriped(offs5)
    idx6 = unstriped(offs6)
    xtu = unpack_weight(xt_words, xt_scales, "e5m2")
    wu = unpack_weight(w_words, w_scales, "e2m1")
    wbu = unpack_weight(wb_words, wb_scales, "e2m1")
    wsu = unpack_weight(ws_words, ws_scales, "e2m1")
    xtidxg = xtu[:, idx]
    a = wu.T @ xtidxg
    xtidx2g = xtu[:, idx2]
    b = wu.T @ xtidx2g
    pw = np.zeros((R, C))
    pw[:, idx3] = a
    hid = np.abs(pw[:, idx4] - b)
    hidq = mxq(hid, 0, "e4m3")
    p = wbu.T @ hidq + wsu.T @ xtidx2g
    y = np.maximum(p[:, idx5], p[:, idx6])
    return y

@@ -1,0 +1,176 @@
+from contextlib import ExitStack
+
+import concourse.mybir as mybir
+
+K, T, J, R, C, N, E = 512, 2048, 256, 512, 512, 256, 128
+FLOPS = 2 * K * R * J * 2 + 2 * R * N * J + 2 * K * N * J
+
+F32 = mybir.dt.float32
+BF16 = mybir.dt.bfloat16
+I32 = mybir.dt.int32
+U32 = mybir.dt.uint32
+U16 = mybir.dt.uint16
+U8 = mybir.dt.uint8
+E4M3 = mybir.dt.float8_e4m3fn_x4
+E5M2 = mybir.dt.float8_e5m2_x4
+E2M1 = mybir.dt.float4_e2m1fn_x4
+ACT = mybir.ActivationFunctionType
+ALU = mybir.AluOpType
+
+P = 128
+PACK = 4
+HALF = J // 2
+
+
+def load_scale_rows(queues, plane, scales):
+    for q, queue in enumerate(queues):
+        queue.dma_start(out=plane[32 * q : 32 * q + 4, :].bitcast(I32), in_=scales[0, 4 * q : 4 * q + 4, :].bitcast(I32))
+
+
+def tile_list_tied_board_skip_bestoftwo_kernel(
+    tc, xt_words, xt_scales, w_words, w_scales, wb_words, wb_scales, ws_words, ws_scales,
+    offs, offs2, offs3, offs4, offs5, offs6, out,
+):
+    nc = tc.nc
+    with ExitStack() as ctx:
+        lists = ctx.enter_context(tc.tile_pool(name="lists", bufs=1))
+        sb = ctx.enter_context(tc.tile_pool(name="sb", bufs=1))
+        psum = ctx.enter_context(tc.psum_pool(name="psum", bufs=1))
+
+        x_words = sb.tile([P, T], U32, name="x_words", align_bytes=64)
+        x_plane = sb.tile([P, T], U8, name="x_plane", align_bytes=64)
+        wt_words = sb.tile([P, 2 * R], U8, name="wt_words", align_bytes=64)
+        wt_plane = sb.tile([P, R], U8, name="wt_plane", align_bytes=64)
+        w_dealt = sb.tile([P, 2 * R], U8, name="w_dealt", align_bytes=64)
+        w_plane_dealt = sb.tile([P, R], U8, name="w_plane_dealt", align_bytes=64)
+        boards = [sb.tile([P, C], F32, name="board%d" % t, align_bytes=64) for t in range(PACK)]
+
+        nc.vector.memset(x_plane[:].bitcast(I32), 0)
+        nc.gpsimd.memset(wt_plane[:].bitcast(I32), 0)
+        for t in range(PACK):
+            nc.vector.memset(boards[t][:], 0.0)
+
+        sources = (offs, offs2, offs3, offs4, offs5, offs6)
+        idx = [lists.tile(list(source.shape), U16, name="list%d" % number) for number, source in enumerate(sources)]
+        nc.sync.dma_start(idx[0][:], sources[0])
+        nc.scalar.dma_start(out=wt_words[:].bitcast(I32), in_=w_words[0].bitcast(I32))
+        nc.scalar.dma_start(out=x_words[:].bitcast(I32), in_=xt_words[0].rearrange("p c i -> p (c i)").bitcast(I32))
+        load_scale_rows([nc.sync] * 4, x_plane, xt_scales)
+        load_scale_rows([nc.sync, nc.sync, nc.gpsimd, nc.gpsimd], wt_plane, w_scales)
+        for number in range(1, 6):
+            nc.sync.dma_start(idx[number][:], sources[number])
+
+        nc.vector.tensor_copy(
+            out=w_dealt[:].bitcast(U16).rearrange("p (t m) -> p t m", t=PACK),
+            in_=wt_words[:].bitcast(U16).rearrange("p (m t) -> p t m", t=PACK),
+        )
+        x1_plane = sb.tile([P, J], U8, name="x1_plane", align_bytes=64)
+        x2_plane = sb.tile([P, J], U8, name="x2_plane", align_bytes=64)
+        x1_words = sb.tile([P, J], U32, name="x1_words", align_bytes=64)
+        x2_words = sb.tile([P, J], U32, name="x2_words", align_bytes=64)
+        nc.vector.tensor_copy(out=x1_plane[:], in_=x_plane[:].indirect(idx[0][:]))
+        nc.vector.tensor_copy(
+            out=w_plane_dealt[:].rearrange("p (t m) -> p t m", t=PACK),
+            in_=wt_plane[:].rearrange("p (m t) -> p t m", t=PACK),
+        )
+        nc.vector.tensor_copy(out=x2_plane[:], in_=x_plane[:].indirect(idx[1][:]))
+        nc.vector.tensor_copy(out=x1_words[:], in_=x_words[:].indirect(idx[0][:]))
+        nc.vector.tensor_copy(out=x2_words[:], in_=x_words[:].indirect(idx[1][:]))
+
+        nc.sync.dma_start(out=wt_words[:, 2 * N :].bitcast(I32), in_=ws_words[0].bitcast(I32))
+        load_scale_rows([nc.sync] * 4, wt_plane[:, N:], ws_scales)
+        nc.sync.dma_start(out=wt_words[:, : 2 * N].bitcast(I32), in_=wb_words[0].bitcast(I32))
+        load_scale_rows([nc.sync] * 4, wt_plane[:, :N], wb_scales)
+
+        def first_stage(acc, t, words, plane):
+            nc.tensor.matmul_mx(
+                out=acc,
+                lhsT=w_dealt[:, 2 * P * t : 2 * P * (t + 1)].bitcast(E2M1),
+                lhsT_scale=w_plane_dealt[:, P * t : P * (t + 1)],
+                rhs=words[:].bitcast(E5M2),
+                rhs_scale=plane[:],
+                start=True,
+                stop=True,
+            )
+
+        banks = ((("a", 0),), (("a", 2),), (("a", 1),), (("b", 0), ("b", 1)), (("a", 3), ("b", 3)), (("b", 2),))
+        operands = {"a": (x1_words, x1_plane), "b": (x2_words, x2_plane)}
+        bank_ps = [psum.tile([P, len(held), J], F32, name="first%d" % n, tag="bank%d" % n) for n, held in enumerate(banks)]
+        bank_sb = [sb.tile([P, len(held), J], F32, name="first_sb%d" % n, align_bytes=64) for n, held in enumerate(banks)]
+        place = {key: (n, s) for n, held in enumerate(banks) for s, key in enumerate(held)}
+        diff = sb.tile([P, PACK, J], F32, name="diff", align_bytes=64)
+
+        def in_sbuf(result, t):
+            n, s = place[(result, t)]
+            return bank_sb[n][:, s, :]
+
+        for held, acc in zip(banks, bank_ps):
+            for s, (result, t) in enumerate(held):
+                first_stage(acc[:, s, :], t, *operands[result])
+        for n in range(3):
+            nc.scalar.activation(out=bank_sb[n][:], in_=bank_ps[n][:], func=ACT.Copy)
+        nc.vector.tensor_copy(out=boards[0][:].indirect(idx[2][:]), in_=in_sbuf("a", 0))
+        nc.scalar.activation(out=boards[2][:].indirect(idx[2][:]), in_=in_sbuf("a", 2), func=ACT.Copy)
+        nc.vector.tensor_copy(out=boards[1][:].indirect(idx[2][:]), in_=in_sbuf("a", 1))
+        for n in range(3, 6):
+            nc.scalar.activation(out=bank_sb[n][:], in_=bank_ps[n][:], func=ACT.Copy)
+        nc.scalar.activation(out=boards[3][:].indirect(idx[2][:]), in_=in_sbuf("a", 3), func=ACT.Copy)
+
+        p_ps = [[psum.tile([P, HALF], F32, name="p_ps%d_%d" % (g, h), tag="bank%d" % (6 + h if g == 0 else h)) for h in range(2)] for g in range(2)]
+        for g in range(2):
+            cols = slice(HALF * g, HALF * (g + 1))
+            for h in range(2):
+                nc.tensor.matmul_mx(
+                    out=p_ps[g][h][:],
+                    lhsT=wt_words[:, 2 * N + 2 * P * h : 2 * N + 2 * P * (h + 1)].bitcast(E2M1),
+                    lhsT_scale=wt_plane[:, N + P * h : N + P * (h + 1)],
+                    rhs=x2_words[:, cols].bitcast(E5M2),
+                    rhs_scale=x2_plane[:, cols],
+                    start=True,
+                    stop=False,
+                )
+        for t in range(PACK - 1):
+            nc.vector.tensor_tensor(out=diff[:, t, :], in0=boards[t][:].indirect(idx[3][:]), in1=in_sbuf("b", t), op=ALU.subtract)
+        for g in range(2):
+            cols = slice(HALF * g, HALF * (g + 1))
+            nc.vector.tensor_tensor(
+                out=diff[:, 3, cols], in0=boards[3][:].indirect(idx[3][:, 8 * g : 8 * (g + 1)]), in1=in_sbuf("b", 3)[:, cols], op=ALU.subtract
+            )
+
+        hid = [sb.tile([P, HALF, PACK], BF16, name="hid%d" % g, align_bytes=64) for g in range(2)]
+        hid_words = sb.tile([P, J], U32, name="hid_words", align_bytes=64)
+        hid_plane = sb.tile([P, J], U8, name="hid_plane", align_bytes=64)
+        part = [diff[:, :, HALF * g : HALF * (g + 1)].rearrange("p t j -> p j t") for g in range(2)]
+        nc.scalar.activation(out=hid[0][:], in_=part[0], func=ACT.Abs)
+        nc.vector.scalar_tensor_tensor(out=hid[1][:], in0=part[1], scalar=-1.0, in1=part[1], op0=ALU.mult, op1=ALU.max)
+        for g in range(2):
+            cols = slice(HALF * g, HALF * (g + 1))
+            nc.vector.quantize_mx(
+                out=hid_words[:, cols].bitcast(E4M3), scales=hid_plane[:, cols], in_=hid[g][:].rearrange("p j t -> p (j t)")
+            )
+        for g in range(2):
+            cols = slice(HALF * g, HALF * (g + 1))
+            for h in range(2):
+                nc.tensor.matmul_mx(
+                    out=p_ps[g][h][:],
+                    lhsT=wt_words[:, 2 * P * h : 2 * P * (h + 1)].bitcast(E2M1),
+                    lhsT_scale=wt_plane[:, P * h : P * (h + 1)],
+                    rhs=hid_words[:, cols].bitcast(E4M3),
+                    rhs_scale=hid_plane[:, cols],
+                    start=False,
+                    stop=True,
+                )
+
+        p_sb = [sb.tile([P, J], F32, name="p_sb%d" % h, align_bytes=64) for h in range(2)]
+        picked = [[sb.tile([P, E], F32, name="pick%d_%d" % (h, s), align_bytes=64) for s in range(2)] for h in range(2)]
+        best = [sb.tile([P, E], F32, name="best%d" % h, align_bytes=64) for h in range(2)]
+        for h in range(2):
+            nc.scalar.activation(out=p_sb[h][:, :HALF], in_=p_ps[0][h][:], func=ACT.Copy)
+        nc.vector.tensor_copy(out=p_sb[0][:, HALF:], in_=p_ps[1][0][:])
+        nc.scalar.activation(out=p_sb[1][:, HALF:], in_=p_ps[1][1][:], func=ACT.Copy)
+        for s in range(2):
+            nc.vector.tensor_copy(out=picked[0][s][:], in_=p_sb[0][:].indirect(idx[4 + s][:]))
+            nc.scalar.activation(out=picked[1][s][:], in_=p_sb[1][:].indirect(idx[4 + s][:]), func=ACT.Copy)
+        for h in range(2):
+            nc.vector.tensor_tensor(out=best[h][:], in0=picked[h][0][:], in1=picked[h][1][:], op=ALU.max)
+            nc.sync.dma_start(out=out[P * h : P * (h + 1), :], in_=best[h][:])

@@ -20,6 +20,7 @@ ALU = mybir.AluOpType
 P = 128
 PACK = 4
 HALF = J // 2
+SPLIT = 160
 
 
 def load_scale_rows(queues, plane, scales):
@@ -45,7 +46,8 @@ def tile_list_tied_board_skip_bestoftwo_kernel(
         w_plane_dealt = sb.tile([P, R], U8, name="w_plane_dealt", align_bytes=64)
         boards = [sb.tile([P, C], F32, name="board%d" % t, align_bytes=64) for t in range(PACK)]
 
-        nc.vector.memset(x_plane[:].bitcast(I32), 0)
+        nc.vector.memset(x_plane[:, : T // 2].bitcast(I32), 0)
+        nc.gpsimd.memset(x_plane[:, T // 2 :].bitcast(I32), 0)
         nc.gpsimd.memset(wt_plane[:].bitcast(I32), 0)
         for t in range(PACK):
             nc.vector.memset(boards[t][:], 0.0)
@@ -53,10 +55,10 @@ def tile_list_tied_board_skip_bestoftwo_kernel(
         sources = (offs, offs2, offs3, offs4, offs5, offs6)
         idx = [lists.tile(list(source.shape), U16, name="list%d" % number) for number, source in enumerate(sources)]
         nc.sync.dma_start(idx[0][:], sources[0])
-        nc.scalar.dma_start(out=wt_words[:].bitcast(I32), in_=w_words[0].bitcast(I32))
-        nc.scalar.dma_start(out=x_words[:].bitcast(I32), in_=xt_words[0].rearrange("p c i -> p (c i)").bitcast(I32))
-        load_scale_rows([nc.sync] * 4, x_plane, xt_scales)
-        load_scale_rows([nc.sync, nc.sync, nc.gpsimd, nc.gpsimd], wt_plane, w_scales)
+        nc.sync.dma_start(out=wt_words[:].bitcast(I32), in_=w_words[0].bitcast(I32))
+        load_scale_rows([nc.sync, nc.sync, nc.scalar, nc.scalar], x_plane, xt_scales)
+        nc.sync.dma_start(out=x_words[:].bitcast(I32), in_=xt_words[0].rearrange("p c i -> p (c i)").bitcast(I32))
+        load_scale_rows([nc.sync] * 4, wt_plane, w_scales)
         for number in range(1, 6):
             nc.sync.dma_start(idx[number][:], sources[number])
 
@@ -69,12 +71,13 @@ def tile_list_tied_board_skip_bestoftwo_kernel(
         x1_words = sb.tile([P, J], U32, name="x1_words", align_bytes=64)
         x2_words = sb.tile([P, J], U32, name="x2_words", align_bytes=64)
         nc.vector.tensor_copy(out=x1_plane[:], in_=x_plane[:].indirect(idx[0][:]))
-        nc.vector.tensor_copy(
-            out=w_plane_dealt[:].rearrange("p (t m) -> p t m", t=PACK),
-            in_=wt_plane[:].rearrange("p (m t) -> p t m", t=PACK),
-        )
-        nc.vector.tensor_copy(out=x2_plane[:], in_=x_plane[:].indirect(idx[1][:]))
         nc.vector.tensor_copy(out=x1_words[:], in_=x_words[:].indirect(idx[0][:]))
+        for slices in (slice(0, 1), slice(1, PACK)):
+            nc.vector.tensor_copy(
+                out=w_plane_dealt[:].rearrange("p (t m) -> p t m", t=PACK)[:, slices, :],
+                in_=wt_plane[:].rearrange("p (m t) -> p t m", t=PACK)[:, slices, :],
+            )
+        nc.vector.tensor_copy(out=x2_plane[:], in_=x_plane[:].indirect(idx[1][:]))
         nc.vector.tensor_copy(out=x2_words[:], in_=x_words[:].indirect(idx[1][:]))
 
         nc.sync.dma_start(out=wt_words[:, 2 * N :].bitcast(I32), in_=ws_words[0].bitcast(I32))
@@ -131,22 +134,29 @@ def tile_list_tied_board_skip_bestoftwo_kernel(
                 )
         for t in range(PACK - 1):
             nc.vector.tensor_tensor(out=diff[:, t, :], in0=boards[t][:].indirect(idx[3][:]), in1=in_sbuf("b", t), op=ALU.subtract)
-        for g in range(2):
-            cols = slice(HALF * g, HALF * (g + 1))
+        for first, last in ((0, SPLIT), (SPLIT, J)):
             nc.vector.tensor_tensor(
-                out=diff[:, 3, cols], in0=boards[3][:].indirect(idx[3][:, 8 * g : 8 * (g + 1)]), in1=in_sbuf("b", 3)[:, cols], op=ALU.subtract
+                out=diff[:, 3, first:last],
+                in0=boards[3][:].indirect(idx[3][:, first // 16 : last // 16]),
+                in1=in_sbuf("b", 3)[:, first:last],
+                op=ALU.subtract,
             )
 
-        hid = [sb.tile([P, HALF, PACK], BF16, name="hid%d" % g, align_bytes=64) for g in range(2)]
+        hid = sb.tile([P, J, PACK], BF16, name="hid", align_bytes=64)
         hid_words = sb.tile([P, J], U32, name="hid_words", align_bytes=64)
         hid_plane = sb.tile([P, J], U8, name="hid_plane", align_bytes=64)
-        part = [diff[:, :, HALF * g : HALF * (g + 1)].rearrange("p t j -> p j t") for g in range(2)]
-        nc.scalar.activation(out=hid[0][:], in_=part[0], func=ACT.Abs)
-        nc.vector.scalar_tensor_tensor(out=hid[1][:], in0=part[1], scalar=-1.0, in1=part[1], op0=ALU.mult, op1=ALU.max)
+        for first, last in ((0, HALF), (HALF, SPLIT)):
+            nc.scalar.activation(
+                out=hid[:, first:last, :].rearrange("p (c i) t -> p c t i", i=2),
+                in_=diff[:, :, first:last].rearrange("p t (c i) -> p c t i", i=2),
+                func=ACT.Abs,
+            )
+        rest = diff[:, :, SPLIT:].rearrange("p t j -> p j t")
+        nc.vector.scalar_tensor_tensor(out=hid[:, SPLIT:, :], in0=rest, scalar=-1.0, in1=rest, op0=ALU.mult, op1=ALU.max)
         for g in range(2):
             cols = slice(HALF * g, HALF * (g + 1))
             nc.vector.quantize_mx(
-                out=hid_words[:, cols].bitcast(E4M3), scales=hid_plane[:, cols], in_=hid[g][:].rearrange("p j t -> p (j t)")
+                out=hid_words[:, cols].bitcast(E4M3), scales=hid_plane[:, cols], in_=hid[:, cols, :].rearrange("p j t -> p (j t)")
             )
         for g in range(2):
             cols = slice(HALF * g, HALF * (g + 1))

from contextlib import ExitStack

import concourse.mybir as mybir

K, T, J, R, C, N, E = 512, 2048, 256, 512, 512, 256, 128
FLOPS = 2 * K * R * J * 2 + 2 * R * N * J + 2 * K * N * J

F32 = mybir.dt.float32
BF16 = mybir.dt.bfloat16
I32 = mybir.dt.int32
U32 = mybir.dt.uint32
U16 = mybir.dt.uint16
U8 = mybir.dt.uint8
E4M3 = mybir.dt.float8_e4m3fn_x4
E5M2 = mybir.dt.float8_e5m2_x4
E2M1 = mybir.dt.float4_e2m1fn_x4
ACT = mybir.ActivationFunctionType
ALU = mybir.AluOpType

P = 128
PACK = 4
HALF = J // 2
SPLIT = 160


def load_scale_rows(queues, plane, scales):
    for q, queue in enumerate(queues):
        queue.dma_start(out=plane[32 * q : 32 * q + 4, :].bitcast(I32), in_=scales[0, 4 * q : 4 * q + 4, :].bitcast(I32))


def tile_list_tied_board_skip_bestoftwo_kernel(
    tc, xt_words, xt_scales, w_words, w_scales, wb_words, wb_scales, ws_words, ws_scales,
    offs, offs2, offs3, offs4, offs5, offs6, out,
):
    nc = tc.nc
    with ExitStack() as ctx:
        lists = ctx.enter_context(tc.tile_pool(name="lists", bufs=1))
        sb = ctx.enter_context(tc.tile_pool(name="sb", bufs=1))
        psum = ctx.enter_context(tc.psum_pool(name="psum", bufs=1))

        x_words = sb.tile([P, T], U32, name="x_words", align_bytes=64)
        x_plane = sb.tile([P, T], U8, name="x_plane", align_bytes=64)
        wt_words = sb.tile([P, 2 * R], U8, name="wt_words", align_bytes=64)
        wt_plane = sb.tile([P, R], U8, name="wt_plane", align_bytes=64)
        w_dealt = sb.tile([P, 2 * R], U8, name="w_dealt", align_bytes=64)
        w_plane_dealt = sb.tile([P, R], U8, name="w_plane_dealt", align_bytes=64)
        boards = [sb.tile([P, C], F32, name="board%d" % t, align_bytes=64) for t in range(PACK)]

        nc.vector.memset(x_plane[:, : T // 2].bitcast(I32), 0)
        nc.gpsimd.memset(x_plane[:, T // 2 :].bitcast(I32), 0)
        nc.gpsimd.memset(wt_plane[:].bitcast(I32), 0)
        for t in range(PACK):
            nc.vector.memset(boards[t][:], 0.0)

        sources = (offs, offs2, offs3, offs4, offs5, offs6)
        idx = [lists.tile(list(source.shape), U16, name="list%d" % number) for number, source in enumerate(sources)]
        nc.sync.dma_start(idx[0][:], sources[0])
        nc.sync.dma_start(out=wt_words[:].bitcast(I32), in_=w_words[0].bitcast(I32))
        load_scale_rows([nc.sync, nc.sync, nc.scalar, nc.scalar], x_plane, xt_scales)
        nc.sync.dma_start(out=x_words[:].bitcast(I32), in_=xt_words[0].rearrange("p c i -> p (c i)").bitcast(I32))
        load_scale_rows([nc.sync] * 4, wt_plane, w_scales)
        for number in range(1, 6):
            nc.sync.dma_start(idx[number][:], sources[number])

        nc.vector.tensor_copy(
            out=w_dealt[:].bitcast(U16).rearrange("p (t m) -> p t m", t=PACK),
            in_=wt_words[:].bitcast(U16).rearrange("p (m t) -> p t m", t=PACK),
        )
        x1_plane = sb.tile([P, J], U8, name="x1_plane", align_bytes=64)
        x2_plane = sb.tile([P, J], U8, name="x2_plane", align_bytes=64)
        x1_words = sb.tile([P, J], U32, name="x1_words", align_bytes=64)
        x2_words = sb.tile([P, J], U32, name="x2_words", align_bytes=64)
        nc.vector.tensor_copy(out=x1_plane[:], in_=x_plane[:].indirect(idx[0][:]))
        nc.vector.tensor_copy(out=x1_words[:], in_=x_words[:].indirect(idx[0][:]))
        for slices in (slice(0, 1), slice(1, PACK)):
            nc.vector.tensor_copy(
                out=w_plane_dealt[:].rearrange("p (t m) -> p t m", t=PACK)[:, slices, :],
                in_=wt_plane[:].rearrange("p (m t) -> p t m", t=PACK)[:, slices, :],
            )
        nc.vector.tensor_copy(out=x2_plane[:], in_=x_plane[:].indirect(idx[1][:]))
        nc.vector.tensor_copy(out=x2_words[:], in_=x_words[:].indirect(idx[1][:]))

        nc.sync.dma_start(out=wt_words[:, 2 * N :].bitcast(I32), in_=ws_words[0].bitcast(I32))
        load_scale_rows([nc.sync] * 4, wt_plane[:, N:], ws_scales)
        nc.sync.dma_start(out=wt_words[:, : 2 * N].bitcast(I32), in_=wb_words[0].bitcast(I32))
        load_scale_rows([nc.sync] * 4, wt_plane[:, :N], wb_scales)

        def first_stage(acc, t, words, plane):
            nc.tensor.matmul_mx(
                out=acc,
                lhsT=w_dealt[:, 2 * P * t : 2 * P * (t + 1)].bitcast(E2M1),
                lhsT_scale=w_plane_dealt[:, P * t : P * (t + 1)],
                rhs=words[:].bitcast(E5M2),
                rhs_scale=plane[:],
                start=True,
                stop=True,
            )

        banks = ((("a", 0),), (("a", 2),), (("a", 1),), (("b", 0), ("b", 1)), (("a", 3), ("b", 3)), (("b", 2),))
        operands = {"a": (x1_words, x1_plane), "b": (x2_words, x2_plane)}
        bank_ps = [psum.tile([P, len(held), J], F32, name="first%d" % n, tag="bank%d" % n) for n, held in enumerate(banks)]
        bank_sb = [sb.tile([P, len(held), J], F32, name="first_sb%d" % n, align_bytes=64) for n, held in enumerate(banks)]
        place = {key: (n, s) for n, held in enumerate(banks) for s, key in enumerate(held)}
        diff = sb.tile([P, PACK, J], F32, name="diff", align_bytes=64)

        def in_sbuf(result, t):
            n, s = place[(result, t)]
            return bank_sb[n][:, s, :]

        for held, acc in zip(banks, bank_ps):
            for s, (result, t) in enumerate(held):
                first_stage(acc[:, s, :], t, *operands[result])
        for n in range(3):
            nc.scalar.activation(out=bank_sb[n][:], in_=bank_ps[n][:], func=ACT.Copy)
        nc.vector.tensor_copy(out=boards[0][:].indirect(idx[2][:]), in_=in_sbuf("a", 0))
        nc.scalar.activation(out=boards[2][:].indirect(idx[2][:]), in_=in_sbuf("a", 2), func=ACT.Copy)
        nc.vector.tensor_copy(out=boards[1][:].indirect(idx[2][:]), in_=in_sbuf("a", 1))
        for n in range(3, 6):
            nc.scalar.activation(out=bank_sb[n][:], in_=bank_ps[n][:], func=ACT.Copy)
        nc.scalar.activation(out=boards[3][:].indirect(idx[2][:]), in_=in_sbuf("a", 3), func=ACT.Copy)

        p_ps = [[psum.tile([P, HALF], F32, name="p_ps%d_%d" % (g, h), tag="bank%d" % (6 + h if g == 0 else h)) for h in range(2)] for g in range(2)]
        for g in range(2):
            cols = slice(HALF * g, HALF * (g + 1))
            for h in range(2):
                nc.tensor.matmul_mx(
                    out=p_ps[g][h][:],
                    lhsT=wt_words[:, 2 * N + 2 * P * h : 2 * N + 2 * P * (h + 1)].bitcast(E2M1),
                    lhsT_scale=wt_plane[:, N + P * h : N + P * (h + 1)],
                    rhs=x2_words[:, cols].bitcast(E5M2),
                    rhs_scale=x2_plane[:, cols],
                    start=True,
                    stop=False,
                )
        for t in range(PACK - 1):
            nc.vector.tensor_tensor(out=diff[:, t, :], in0=boards[t][:].indirect(idx[3][:]), in1=in_sbuf("b", t), op=ALU.subtract)
        for first, last in ((0, SPLIT), (SPLIT, J)):
            nc.vector.tensor_tensor(
                out=diff[:, 3, first:last],
                in0=boards[3][:].indirect(idx[3][:, first // 16 : last // 16]),
                in1=in_sbuf("b", 3)[:, first:last],
                op=ALU.subtract,
            )

        hid = sb.tile([P, J, PACK], BF16, name="hid", align_bytes=64)
        hid_words = sb.tile([P, J], U32, name="hid_words", align_bytes=64)
        hid_plane = sb.tile([P, J], U8, name="hid_plane", align_bytes=64)
        for first, last in ((0, HALF), (HALF, SPLIT)):
            nc.scalar.activation(
                out=hid[:, first:last, :].rearrange("p (c i) t -> p c t i", i=2),
                in_=diff[:, :, first:last].rearrange("p t (c i) -> p c t i", i=2),
                func=ACT.Abs,
            )
        rest = diff[:, :, SPLIT:].rearrange("p t j -> p j t")
        nc.vector.scalar_tensor_tensor(out=hid[:, SPLIT:, :], in0=rest, scalar=-1.0, in1=rest, op0=ALU.mult, op1=ALU.max)
        for g in range(2):
            cols = slice(HALF * g, HALF * (g + 1))
            nc.vector.quantize_mx(
                out=hid_words[:, cols].bitcast(E4M3), scales=hid_plane[:, cols], in_=hid[:, cols, :].rearrange("p j t -> p (j t)")
            )
        for g in range(2):
            cols = slice(HALF * g, HALF * (g + 1))
            for h in range(2):
                nc.tensor.matmul_mx(
                    out=p_ps[g][h][:],
                    lhsT=wt_words[:, 2 * P * h : 2 * P * (h + 1)].bitcast(E2M1),
                    lhsT_scale=wt_plane[:, P * h : P * (h + 1)],
                    rhs=hid_words[:, cols].bitcast(E4M3),
                    rhs_scale=hid_plane[:, cols],
                    start=False,
                    stop=True,
                )

        p_sb = [sb.tile([P, J], F32, name="p_sb%d" % h, align_bytes=64) for h in range(2)]
        picked = [[sb.tile([P, E], F32, name="pick%d_%d" % (h, s), align_bytes=64) for s in range(2)] for h in range(2)]
        best = [sb.tile([P, E], F32, name="best%d" % h, align_bytes=64) for h in range(2)]
        for h in range(2):
            nc.scalar.activation(out=p_sb[h][:, :HALF], in_=p_ps[0][h][:], func=ACT.Copy)
        nc.vector.tensor_copy(out=p_sb[0][:, HALF:], in_=p_ps[1][0][:])
        nc.scalar.activation(out=p_sb[1][:, HALF:], in_=p_ps[1][1][:], func=ACT.Copy)
        for s in range(2):
            nc.vector.tensor_copy(out=picked[0][s][:], in_=p_sb[0][:].indirect(idx[4 + s][:]))
            nc.scalar.activation(out=picked[1][s][:], in_=p_sb[1][:].indirect(idx[4 + s][:]), func=ACT.Copy)
        for h in range(2):
            nc.vector.tensor_tensor(out=best[h][:], in0=picked[h][0][:], in1=picked[h][1][:], op=ALU.max)
            nc.sync.dma_start(out=out[P * h : P * (h + 1), :], in_=best[h][:])
